import numpy as np, ml_dtypes
CORES = [10,18,34,42,58,66,82,90,98,106]
N = 10
F = 512
def setup_inputs(rng):
    x = (rng.standard_normal((N, 128, 128), dtype=np.float32) / 11).astype(ml_dtypes.bfloat16)
    w = rng.standard_normal((128, F), dtype=np.float32).astype(ml_dtypes.bfloat16)
    return {"x": x, "xt": x.transpose(0, 2, 1).copy(), "w": np.broadcast_to(w, (N, 128, F)).copy()}
def setup_inputs_big(rng):
    d = setup_inputs(rng)
    for k in ("x", "xt", "w"): d[k] = (d[k].astype(np.float32) * 1024.0).astype(d[k].dtype)
    return d
def setup_inputs_small(rng):
    d = setup_inputs(rng)
    for k in ("x", "xt", "w"): d[k] = (d[k].astype(np.float32) * (1 / 1024.0)).astype(d[k].dtype)
    return d
def setup_inputs_apart(rng):
    d = setup_inputs(rng)
    f = (10.0 ** rng.permutation(np.linspace(-1.5, 1.5, N))).astype(np.float32).reshape(N, 1, 1)
    for k in ("x", "xt"): d[k] = (d[k].astype(np.float32) * f).astype(d[k].dtype)
    return d
def tie_inputs(x):
    x = dict(x)
    x["xt"] = x["x"].transpose(0, 2, 1).copy(); x["w"] = np.broadcast_to(x["w"][0], x["w"].shape).copy()
    return x
def reference(x, xt, w):
    X, XT, W = x.astype(np.float64), xt.astype(np.float64), w.astype(np.float64)
    s = sum(X[j].T @ (XT[j].T @ W[j]) for j in range(N)).astype(ml_dtypes.bfloat16 if x.dtype != np.float64 else np.float64)
    return {"y": np.broadcast_to(s, (N,) + s.shape)}

@@ -1,0 +1,67 @@
+from concourse.bass import DstId, RemoteDMATransfer
+
+N = 10
+D = 128
+F = 512
+
+SCRATCH = {
+    "xall": ("sbuf", [128, N * D], "bfloat16"),
+    "wsb": ("sbuf", [128, F], "bfloat16"),
+    "gsb": ("sbuf", [128, D], "bfloat16"),
+    "ysb": ("sbuf", [128, F], "bfloat16"),
+    "gps": ("psum", [128, 512], "float32"),
+    "yps": ("psum", [128, 512], "float32"),
+}
+SEMAPHORES = ["ldx", "ldw", "sent", "gdone", "gcp", "ydone", "ycp", "stored"] + ["arr%d" % j for j in range(N)]
+
+
+def rank_program(g, core, T, topo):
+    rank = T.rank_of(core)
+    if rank is None:
+        return
+    S = T.sem
+
+    def slot(j):
+        return T.xall[:, j * D:(j + 1) * D]
+
+    g.sync.dma_start(slot(rank), T.x[:, :]).then_inc(S.ldx, 16)
+    g.scalar.dma_start(T.wsb[:, :], T.w[:, :]).then_inc(S.ldw, 16)
+
+    order = [(rank + k) % N for k in range(1, N)]
+    mask = -1
+    ids = []
+    for j in order:
+        dst = T.cores[j]
+        assert topo.may_write(core, dst)
+        mask &= topo.mask(core, dst)
+        rid, pid, _ = topo.addr(dst)
+        ids.append(DstId(rid=rid, pnc=pid))
+    engines = bin(mask).count("1")
+    g.wait_ge(S.ldx, 16)
+    g.remote_dma_fused(
+        [RemoteDMATransfer(dst_ids=ids, dma_engine_mask=mask, remote_sem=S["arr%d" % rank],
+                           srcs=[slot(rank)], dsts=[slot(rank) for _ in order])],
+        local_sem=S.sent)
+
+    te, ve = g.tensor, g.vector
+    te.wait_ge(S.ldx, 16)
+    te.matmul(T.gps[:, 0:D], slot(rank), slot(rank), True, False)
+    arrivals = [(rank - k) % N for k in range(1, N)]
+    for i, j in enumerate(arrivals):
+        te.wait_ge(S["arr%d" % j], engines)
+        mm = te.matmul(T.gps[:, 0:D], slot(j), slot(j), False, i == len(arrivals) - 1)
+    mm.then_inc(S.gdone, 1)
+
+    ve.wait_ge(S.gdone, 1)
+    ve.tensor_copy(T.gsb[:, :], T.gps[:, 0:D]).then_inc(S.gcp, 1)
+
+    te.wait_ge(S.ldw, 16)
+    te.wait_ge(S.gcp, 1)
+    te.matmul(T.yps[:, :], T.gsb[:, :], T.wsb[:, :], True, True).then_inc(S.ydone, 1)
+    ve.wait_ge(S.ydone, 1)
+    ve.tensor_copy(T.ysb[:, :], T.yps[:, :]).then_inc(S.ycp, 1)
+
+    g.sync.wait_ge(S.ycp, 1)
+    g.sync.dma_start(T.y[:, :], T.ysb[:, :]).then_inc(S.stored, 16)
+    g.sync.wait_ge(S.stored, 16)
+    g.wait_ge(S.sent, engines)

@@ -3,16 +3,33 @@ from concourse.bass import DstId, RemoteDMATransfer
 N = 10
 D = 128
 F = 512
+PIECES = [(0, 64), (64, 192), (192, 384), (384, 512)]
+CALLS = [5, 3, 1]
 
 SCRATCH = {
     "xall": ("sbuf", [128, N * D], "bfloat16"),
+    "xd": ("dram", [128, D], "bfloat16"),
     "wsb": ("sbuf", [128, F], "bfloat16"),
     "gsb": ("sbuf", [128, D], "bfloat16"),
     "ysb": ("sbuf", [128, F], "bfloat16"),
     "gps": ("psum", [128, 512], "float32"),
-    "yps": ("psum", [128, 512], "float32"),
+    "yps0": ("psum", [128, 512], "float32"),
+    "yps1": ("psum", [128, 512], "float32"),
+    "yps2": ("psum", [128, 512], "float32"),
+    "yps3": ("psum", [128, 512], "float32"),
 }
-SEMAPHORES = ["ldx", "ldw", "sent", "gdone", "gcp", "ydone", "ycp", "stored"] + ["arr%d" % j for j in range(N)]
+SEMAPHORES = (["ldx", "ldd", "ldw", "sent", "gdone", "gcp", "st_sync", "st_scalar"]
+              + ["arr%d" % j for j in range(N)]
+              + ["m%d" % i for i in range(len(PIECES))] + ["c%d" % i for i in range(len(PIECES))])
+
+
+def send_order(i, cores, topo):
+    me = topo.chip(cores[i])
+    own = [j for j in range(len(cores)) if j == i or topo.same_plane(topo.chip(cores[j]), me)]
+    far = [j for j in range(len(cores)) if j not in own]
+    p = own.index(i)
+    return ([far[(p + k) % len(far)] for k in range(len(far))]
+            + [own[(p + k) % len(own)] for k in range(1, len(own))])
 
 
 def rank_program(g, core, T, topo):
@@ -24,10 +41,11 @@ def rank_program(g, core, T, topo):
     def slot(j):
         return T.xall[:, j * D:(j + 1) * D]
 
+    g.sync.dma_start(T.xd[:, :], T.x[:, :]).then_inc(S.ldd, 16)
     g.sync.dma_start(slot(rank), T.x[:, :]).then_inc(S.ldx, 16)
-    g.scalar.dma_start(T.wsb[:, :], T.w[:, :]).then_inc(S.ldw, 16)
+    g.sync.dma_start(T.wsb[:, :], T.w[:, :]).then_inc(S.ldw, 16)
 
-    order = [(rank + k) % N for k in range(1, N)]
+    order = send_order(rank, T.cores, topo)
     mask = -1
     ids = []
     for j in order:
@@ -37,16 +55,20 @@ def rank_program(g, core, T, topo):
         rid, pid, _ = topo.addr(dst)
         ids.append(DstId(rid=rid, pnc=pid))
     engines = bin(mask).count("1")
-    g.wait_ge(S.ldx, 16)
-    g.remote_dma_fused(
-        [RemoteDMATransfer(dst_ids=ids, dma_engine_mask=mask, remote_sem=S["arr%d" % rank],
-                           srcs=[slot(rank)], dsts=[slot(rank) for _ in order])],
-        local_sem=S.sent)
+    g.wait_ge(S.ldd, 16)
+    at = 0
+    for n in CALLS:
+        g.remote_dma_fused(
+            [RemoteDMATransfer(dst_ids=ids[at:at + n], dma_engine_mask=mask, remote_sem=S["arr%d" % rank],
+                               srcs=[T.xd[:, :]], dsts=[slot(rank) for _ in range(n)])],
+            local_sem=S.sent)
+        at += n
 
     te, ve = g.tensor, g.vector
     te.wait_ge(S.ldx, 16)
     te.matmul(T.gps[:, 0:D], slot(rank), slot(rank), True, False)
-    arrivals = [(rank - k) % N for k in range(1, N)]
+    arrivals = sorted([j for j in range(N) if j != rank],
+                      key=lambda j: send_order(j, T.cores, topo).index(rank))
     for i, j in enumerate(arrivals):
         te.wait_ge(S["arr%d" % j], engines)
         mm = te.matmul(T.gps[:, 0:D], slot(j), slot(j), False, i == len(arrivals) - 1)
@@ -57,11 +79,17 @@ def rank_program(g, core, T, topo):
 
     te.wait_ge(S.ldw, 16)
     te.wait_ge(S.gcp, 1)
-    te.matmul(T.yps[:, :], T.gsb[:, :], T.wsb[:, :], True, True).then_inc(S.ydone, 1)
-    ve.wait_ge(S.ydone, 1)
-    ve.tensor_copy(T.ysb[:, :], T.yps[:, :]).then_inc(S.ycp, 1)
-
-    g.sync.wait_ge(S.ycp, 1)
-    g.sync.dma_start(T.y[:, :], T.ysb[:, :]).then_inc(S.stored, 16)
-    g.sync.wait_ge(S.stored, 16)
-    g.wait_ge(S.sent, engines)
+    queues = [(g.sync, S.st_sync), (g.scalar, S.st_scalar)]
+    issued = [0, 0]
+    for i, (a, b) in enumerate(PIECES):
+        ps = T["yps%d" % i][:, 0:b - a]
+        te.matmul(ps, T.gsb[:, :], T.wsb[:, a:b], True, True).then_inc(S["m%d" % i], 1)
+        ve.wait_ge(S["m%d" % i], 1)
+        ve.tensor_copy(T.ysb[:, a:b], ps).then_inc(S["c%d" % i], 1)
+        q, st = queues[i % 2]
+        q.wait_ge(S["c%d" % i], 1)
+        q.dma_start(T.y[:, a:b], T.ysb[:, a:b]).then_inc(st, 16)
+        issued[i % 2] += 16
+    for (q, st), n in zip(queues, issued):
+        q.wait_ge(st, n)
+    g.wait_ge(S.sent, engines * len(CALLS))

from concourse.bass import DstId, RemoteDMATransfer

N = 10
D = 128
F = 512
PIECES = [(0, 64), (64, 192), (192, 384), (384, 512)]
CALLS = [5, 3, 1]

SCRATCH = {
    "xall": ("sbuf", [128, N * D], "bfloat16"),
    "xd": ("dram", [128, D], "bfloat16"),
    "wsb": ("sbuf", [128, F], "bfloat16"),
    "gsb": ("sbuf", [128, D], "bfloat16"),
    "ysb": ("sbuf", [128, F], "bfloat16"),
    "gps": ("psum", [128, 512], "float32"),
    "yps0": ("psum", [128, 512], "float32"),
    "yps1": ("psum", [128, 512], "float32"),
    "yps2": ("psum", [128, 512], "float32"),
    "yps3": ("psum", [128, 512], "float32"),
}
SEMAPHORES = (["ldx", "ldd", "ldw", "sent", "gdone", "gcp", "st_sync", "st_scalar"]
              + ["arr%d" % j for j in range(N)]
              + ["m%d" % i for i in range(len(PIECES))] + ["c%d" % i for i in range(len(PIECES))])


def send_order(i, cores, topo):
    me = topo.chip(cores[i])
    own = [j for j in range(len(cores)) if j == i or topo.same_plane(topo.chip(cores[j]), me)]
    far = [j for j in range(len(cores)) if j not in own]
    p = own.index(i)
    return ([far[(p + k) % len(far)] for k in range(len(far))]
            + [own[(p + k) % len(own)] for k in range(1, len(own))])


def rank_program(g, core, T, topo):
    rank = T.rank_of(core)
    if rank is None:
        return
    S = T.sem

    def slot(j):
        return T.xall[:, j * D:(j + 1) * D]

    g.sync.dma_start(T.xd[:, :], T.x[:, :]).then_inc(S.ldd, 16)
    g.sync.dma_start(slot(rank), T.x[:, :]).then_inc(S.ldx, 16)
    g.sync.dma_start(T.wsb[:, :], T.w[:, :]).then_inc(S.ldw, 16)

    order = send_order(rank, T.cores, topo)
    mask = -1
    ids = []
    for j in order:
        dst = T.cores[j]
        assert topo.may_write(core, dst)
        mask &= topo.mask(core, dst)
        rid, pid, _ = topo.addr(dst)
        ids.append(DstId(rid=rid, pnc=pid))
    engines = bin(mask).count("1")
    g.wait_ge(S.ldd, 16)
    at = 0
    for n in CALLS:
        g.remote_dma_fused(
            [RemoteDMATransfer(dst_ids=ids[at:at + n], dma_engine_mask=mask, remote_sem=S["arr%d" % rank],
                               srcs=[T.xd[:, :]], dsts=[slot(rank) for _ in range(n)])],
            local_sem=S.sent)
        at += n

    te, ve = g.tensor, g.vector
    te.wait_ge(S.ldx, 16)
    te.matmul(T.gps[:, 0:D], slot(rank), slot(rank), True, False)
    arrivals = sorted([j for j in range(N) if j != rank],
                      key=lambda j: send_order(j, T.cores, topo).index(rank))
    for i, j in enumerate(arrivals):
        te.wait_ge(S["arr%d" % j], engines)
        mm = te.matmul(T.gps[:, 0:D], slot(j), slot(j), False, i == len(arrivals) - 1)
    mm.then_inc(S.gdone, 1)

    ve.wait_ge(S.gdone, 1)
    ve.tensor_copy(T.gsb[:, :], T.gps[:, 0:D]).then_inc(S.gcp, 1)

    te.wait_ge(S.ldw, 16)
    te.wait_ge(S.gcp, 1)
    queues = [(g.sync, S.st_sync), (g.scalar, S.st_scalar)]
    issued = [0, 0]
    for i, (a, b) in enumerate(PIECES):
        ps = T["yps%d" % i][:, 0:b - a]
        te.matmul(ps, T.gsb[:, :], T.wsb[:, a:b], True, True).then_inc(S["m%d" % i], 1)
        ve.wait_ge(S["m%d" % i], 1)
        ve.tensor_copy(T.ysb[:, a:b], ps).then_inc(S["c%d" % i], 1)
        q, st = queues[i % 2]
        q.wait_ge(S["c%d" % i], 1)
        q.dma_start(T.y[:, a:b], T.ysb[:, a:b]).then_inc(st, 16)
        issued[i % 2] += 16
    for (q, st), n in zip(queues, issued):
        q.wait_ge(st, n)
    g.wait_ge(S.sent, engines * len(CALLS))
